import numpy as np
import ml_dtypes


def mxq(x, axis, fmt="e4m3"):
    dtype, down = {"e4m3": (ml_dtypes.float8_e4m3fn, 7), "e5m2": (ml_dtypes.float8_e5m2, 14)}[fmt]
    v = np.moveaxis(np.asarray(x, np.float32).astype(ml_dtypes.bfloat16).astype(np.float64), axis, -1)
    blocks = v.reshape(v.shape[:-1] + (-1, 32))
    amax = np.abs(blocks).max(-1, keepdims=True)
    byte = np.maximum(np.where(amax > 0, np.frexp(amax)[1] - 1 + 127, 0) - down, 1)
    scale = np.exp2(byte - 127.0)
    codes = (blocks / scale).astype(np.float32).astype(dtype).astype(np.float64)
    return np.moveaxis((codes * scale).reshape(v.shape), -1, axis)


WIDE = False


def mx_kscale(k):
    if not WIDE:
        return np.ones(k)
    levels = np.array([30, -30])
    if k % 512:
        return np.exp2(np.random.permutation(np.resize(levels, k // 32))).repeat(32)
    a = np.empty((k // 512, 16))
    for p in range(k // 512):
        a[p, :8] = np.random.permutation(np.resize(levels, 8))
        for g in range(8):
            far = levels[np.abs(levels - a[p, g]) >= 10]
            a[p, g + 8] = far[np.random.randint(len(far))]
    return np.exp2(a.ravel()).repeat(32)


def f64(x):
    return np.asarray(x).astype(np.float64)


def striped(idx):
    return np.tile(np.asarray(idx).reshape(-1, 16).T, (8, 1)).astype(np.uint16)


def unstriped(offs):
    return offs[:16].T.reshape(-1).astype(np.int64)


E2M1 = np.array([0.0, 0.5, 1.0, 1.5, 2.0, 3.0, 4.0, 6.0, -0.0, -0.5, -1.0, -1.5, -2.0, -3.0, -4.0, -6.0])


def pack_weight(w, fmt):
    k, n = w.shape
    w = f64(np.asarray(w, np.float32).astype(ml_dtypes.bfloat16)).reshape(k // 32, 32, n)
    amax = np.abs(w).max(1)
    if fmt == "e4m3":
        byte = np.frexp(amax)[1] - 1 + 127 - 7
    else:
        mant, ex = np.frexp(amax / 6.0)
        byte = np.where(mant > 0.5, ex, ex - 1) + 127
    byte = np.clip(np.where(amax > 0, byte, 1), 1, 254)
    scaled = (w * np.exp2(127.0 - byte)[:, None, :]).reshape(k, n).astype(np.float32)
    by_word = np.ascontiguousarray(scaled.reshape(k // 512, 128, 4, n).transpose(0, 1, 3, 2))
    if fmt == "e4m3":
        words = by_word.astype(ml_dtypes.float8_e4m3fn).view(np.uint8)
    else:
        c = by_word.astype(ml_dtypes.float4_e2m1fn).view(np.uint8) & 0xF
        words = (c[..., 0::2] | (c[..., 1::2] << 4)).reshape(k // 512, 128, 2 * n)
    return np.ascontiguousarray(words), np.ascontiguousarray(byte.astype(np.uint8).reshape(k // 512, 16, n))


def unpack_weight(words, scales, fmt):
    g, _, n = scales.shape
    words = np.ascontiguousarray(words).reshape(g, 128, n, -1)
    if fmt == "e4m3":
        vals = words.view(ml_dtypes.float8_e4m3fn).astype(np.float64)
    else:
        nib = np.empty((g, 128, n, 4), np.uint8)
        nib[..., 0::2] = words & 0xF
        nib[..., 1::2] = words >> 4
        vals = E2M1[nib]
    vals = vals * np.repeat(np.exp2(scales.astype(np.float64) - 127.0), 8, axis=1)[..., None]
    return vals.transpose(0, 1, 3, 2).reshape(g * 512, n)


K, T, J, R, G, N, Z = 512, 512, 256, 512, 64, 256, 512


def setup_inputs():
    n = np.random.standard_normal
    idx = np.random.permutation(T)[:J]
    idx2 = np.random.permutation(T)[:J]
    idx3 = np.random.permutation(Z)[:J]
    fk = mx_kscale(K)
    fr = mx_kscale(R)
    wp = pack_weight(n((K, R)) * 1 / np.sqrt(K) * fk[:, None], "e2m1")
    wbp = pack_weight(n((R, N)) * 1 / np.sqrt(R) / fr[:, None], "e2m1")
    return {
        "xf": (n((K, T))).astype(np.float32),
        "fk": (np.random.uniform(0.5, 2.0, (K, 1)) / fk[:, None]).astype(np.float32),
        "w_words": wp[0],
        "w_scales": wp[1],
        "us": (np.random.uniform(0.5, 1.5, (1, R)) * fr).astype(np.float32),
        "wb_words": wbp[0],
        "wb_scales": wbp[1],
        "tz": (n((N, Z))).astype(np.float32),
        "offs": striped(idx),
        "offs2": striped(idx2),
        "offs3": striped(idx3),
    }


def reference(xf, fk, w_words, w_scales, us, wb_words, wb_scales, tz, offs, offs2, offs3):
    idx = unstriped(offs)
    idx2 = unstriped(offs2)
    idx3 = unstriped(offs3)
    wu = unpack_weight(w_words, w_scales, "e2m1")
    wbu = unpack_weight(wb_words, wb_scales, "e2m1")
    u = (f64(xf)[:, idx] - f64(xf)[:, idx2]) * f64(fk)
    uq = mxq(u, 0, "e4m3")
    a = uq.T @ wu
    m1 = a.reshape(J, G, R // G).max(axis=2)
    m2 = np.repeat(m1, R // G, axis=1)
    hr = np.maximum(a - 0.5 * m2, 0.0) * f64(us)
    hid = hr.T
    hidq = mxq(hid, 0, "e5m2")
    p = wbu.T @ hidq
    y = p * f64(tz)[:, idx3]
    return y

@@ -1,0 +1,196 @@
+from contextlib import ExitStack
+
+import concourse.mybir as mybir
+from concourse.masks import make_identity
+
+K, T, J, R, G, N, Z = 512, 512, 256, 512, 64, 256, 512
+P = 128
+PACK = 4
+BUNDLE = R // G
+SCALAR_SLOTS = 64
+FLOPS = 2 * J * K * R + 2 * R * N * J
+
+F32 = mybir.dt.float32
+BF16 = mybir.dt.bfloat16
+I32 = mybir.dt.int32
+U32 = mybir.dt.uint32
+U16 = mybir.dt.uint16
+U8 = mybir.dt.uint8
+E4M3 = mybir.dt.float8_e4m3fn_x4
+E5M2 = mybir.dt.float8_e5m2_x4
+E2M1 = mybir.dt.float4_e2m1fn_x4
+ALU = mybir.AluOpType
+ACT = mybir.ActivationFunctionType
+AXIS = mybir.AxisListType
+
+
+def tile_list_rows_pickgaps_grouppeaks_timeslook_kernel(
+    tc, xf, fk, w_words, w_scales, us, wb_words, wb_scales, tz, offs, offs2, offs3, out
+):
+    nc = tc.nc
+    JT = J // P
+    NT = N // P
+    HALF = R // 2
+
+    with ExitStack() as ctx:
+        keep = ctx.enter_context(tc.tile_pool(name="keep", bufs=1))
+        psum = ctx.enter_context(tc.psum_pool(name="psum", bufs=1))
+
+        first = keep.tile([P, J // 16], U16, name="first")
+        second = keep.tile([P, J // 16], U16, name="second")
+        third = keep.tile([P, J // 16], U16, name="third")
+        x_rows = [keep.tile([P, T], F32, name="x_rows%d" % i) for i in range(PACK)]
+        fk_sb = keep.tile([P, PACK], F32, name="fk_sb")
+        us_sb = keep.tile([P, PACK], F32, name="us_sb")
+        w_sb = keep.tile([P, 2 * R], U8, name="w_sb", align_bytes=64)
+        wb_sb = keep.tile([P, 2 * N], U8, name="wb_sb", align_bytes=64)
+        w_sc = keep.tile([P, R], U8, name="w_sc", align_bytes=64)
+        wb_sc = keep.tile([P, N], U8, name="wb_sc", align_bytes=64)
+        tz_rows = [keep.tile([P, Z], F32, name="tz_rows%d" % a) for a in range(NT)]
+        ident = keep.tile([P, P], F32, name="ident")
+
+        warm = keep.tile([P, 1], F32, name="warm")
+        warmed = keep.tile([P, 1], F32, name="warmed")
+        nc.vector.memset(warm[:], 0.0)
+        nc.scalar.activation(warmed[:], warm[:], ACT.Copy)
+        make_identity(nc, ident[:])
+        nc.vector.memset(w_sc[:].bitcast(I32), 0)
+        nc.vector.memset(wb_sc[:].bitcast(I32), 0)
+
+        x_view = xf.rearrange("(p i) t -> p i t", i=PACK)
+        nc.sync.dma_start(second[:], offs2)
+        nc.sync.dma_start(x_rows[0][:], x_view[:, 0, :])
+        nc.sync.dma_start(first[:], offs)
+        for i in range(1, PACK):
+            nc.sync.dma_start(x_rows[i][:], x_view[:, i, :])
+        nc.sync.dma_start(fk_sb[:], fk.rearrange("(p i) o -> p (i o)", i=PACK))
+        nc.sync.dma_start(w_sb[:].bitcast(I32), w_words[0].bitcast(I32))
+        for q in range(4):
+            nc.sync.dma_start(
+                w_sc[32 * q : 32 * q + 4, :].bitcast(I32), w_scales[0, 4 * q : 4 * q + 4, :].bitcast(I32)
+            )
+        nc.sync.dma_start(us_sb[:], us.rearrange("o (p i) -> p (o i)", i=PACK))
+        nc.sync.dma_start(third[:], offs3)
+        for a in range(NT):
+            nc.sync.dma_start(tz_rows[a][:], tz[a * P : (a + 1) * P, :])
+        nc.sync.dma_start(wb_sb[:].bitcast(I32), wb_words[0].bitcast(I32))
+        for q in range(4):
+            nc.sync.dma_start(
+                wb_sc[32 * q : 32 * q + 4, :].bitcast(I32), wb_scales[0, 4 * q : 4 * q + 4, :].bitcast(I32)
+            )
+
+        taken = keep.tile([P, PACK, J], F32, name="taken")
+        gaps = keep.tile([P, PACK, J], F32, name="gaps")
+        for i in range(PACK):
+            width = P if i in (0, PACK - 1) else J
+            for j0 in range(0, J, width):
+                slots = slice(j0, j0 + width)
+                cols = slice(j0 // 16, (j0 + width) // 16)
+                nc.scalar.activation(taken[:, i, slots], x_rows[i][:].indirect(second[:, cols]), ACT.Copy)
+                nc.vector.tensor_tensor(
+                    gaps[:, i, slots], x_rows[i][:].indirect(first[:, cols]), taken[:, i, slots], ALU.subtract
+                )
+
+        u_bf = [keep.tile([P, P * PACK], BF16, name="u_bf%d" % h, align_bytes=64) for h in range(JT)]
+        u_codes = [keep.tile([P, P], U32, name="u_codes%d" % h, align_bytes=64) for h in range(JT)]
+        u_sc = [keep.tile([P, P], U8, name="u_sc%d" % h, align_bytes=64) for h in range(JT)]
+        for i in range(PACK):
+            nc.scalar.activation(
+                u_bf[0][:].rearrange("p (j i) -> p i j", i=PACK)[:, i, 0:SCALAR_SLOTS],
+                gaps[:, i, 0:SCALAR_SLOTS],
+                ACT.Copy,
+                scale=fk_sb[:, i : i + 1],
+            )
+        def weave(j0):
+            h, c0 = divmod(j0, P)
+            nc.vector.tensor_tensor(
+                u_bf[h][:, PACK * c0 : PACK * (c0 + 64)].rearrange("p (c s i) -> p c i s", s=4, i=PACK),
+                gaps[:, :, j0 : j0 + 64].rearrange("p i (c s) -> p c i s", s=4),
+                fk_sb[:].unsqueeze(1).unsqueeze(3).to_broadcast([P, 16, PACK, 4]),
+                ALU.mult,
+            )
+
+        def quantise_gaps(h):
+            nc.vector.quantize_mx(out=u_codes[h][:].bitcast(E4M3), scales=u_sc[h][:], in_=u_bf[h][:])
+
+        weave(64)
+        weave(128)
+        quantise_gaps(0)
+        weave(192)
+        quantise_gaps(1)
+
+        looked = keep.tile([P, NT, J], F32, name="looked")
+        for a in range(NT):
+            nc.scalar.activation(looked[:, a, :], tz_rows[a][:].indirect(third[:]), ACT.Copy)
+
+        a_ps = [[psum.tile([P, HALF], F32, name="a_ps%d%d" % (h, s)) for s in range(2)] for h in range(JT)]
+        peaks = [keep.tile([P, G], F32, name="peaks%d" % h) for h in range(JT)]
+        above = [keep.tile([P, PACK, P], F32, name="above%d" % h) for h in range(JT)]
+        for h in range(JT):
+            for s in range(2):
+                nc.tensor.matmul_mx(
+                    out=a_ps[h][s][:],
+                    lhsT=u_codes[h][:].bitcast(E4M3),
+                    lhsT_scale=u_sc[h][:],
+                    rhs=w_sb[:, 2 * s * HALF : 2 * (s + 1) * HALF].bitcast(E2M1),
+                    rhs_scale=w_sc[:, s * HALF : (s + 1) * HALF],
+                    start=True,
+                    stop=True,
+                )
+        GH = G // 2
+        for h in range(JT):
+            for s in range(2):
+                nc.vector.tensor_reduce(
+                    peaks[h][:, s * GH : (s + 1) * GH],
+                    a_ps[h][s][:].rearrange("p (g e) -> p g e", e=BUNDLE),
+                    AXIS.X,
+                    ALU.max,
+                )
+        for h in range(JT):
+            for pair in range(2):
+                for s in range(2):
+                    nc.vector.scalar_tensor_tensor(
+                        above[h][:, 2 * pair : 2 * pair + 2, s * 64 : (s + 1) * 64].rearrange("p i q -> p q i"),
+                        peaks[h][:, s * GH : (s + 1) * GH].unsqueeze(2).to_broadcast([P, GH, 4]),
+                        -0.5,
+                        a_ps[h][s][:].rearrange("p (q i) -> p q i", i=PACK)[:, :, 2 * pair : 2 * pair + 2],
+                        ALU.mult,
+                        ALU.add,
+                    )
+
+        turned = [psum.tile([P, PACK, P], F32, name="turned%d" % h) for h in range(JT)]
+        h_bf = [keep.tile([P, P * PACK], BF16, name="h_bf%d" % h, align_bytes=64) for h in range(JT)]
+        h_codes = [keep.tile([P, P], U32, name="h_codes%d" % h, align_bytes=64) for h in range(JT)]
+        h_sc = [keep.tile([P, P], U8, name="h_sc%d" % h, align_bytes=64) for h in range(JT)]
+        for h in range(JT):
+            for i in range(PACK):
+                nc.tensor.transpose(turned[h][:, i, :], above[h][:, i, :], ident[:])
+        for h in range(JT):
+            nc.vector.scalar_tensor_tensor(
+                h_bf[h][:].rearrange("p (j i) -> p j i", i=PACK),
+                turned[h][:].rearrange("p i j -> p j i"),
+                0.0,
+                us_sb[:].unsqueeze(1).to_broadcast([P, P, PACK]),
+                ALU.max,
+                ALU.mult,
+            )
+        for h in range(JT):
+            nc.vector.quantize_mx(out=h_codes[h][:].bitcast(E5M2), scales=h_sc[h][:], in_=h_bf[h][:])
+
+        p_ps = [psum.tile([P, NT, P], F32, name="p_ps%d" % h) for h in range(JT)]
+        res = [keep.tile([P, NT, P], F32, name="res%d" % h) for h in range(JT)]
+        out_view = out.rearrange("(a p) j -> p a j", p=P)
+        for h in range(JT):
+            for a in range(NT):
+                nc.tensor.matmul_mx(
+                    out=p_ps[h][:, a, :],
+                    lhsT=wb_sb[:, 2 * a * P : 2 * (a + 1) * P].bitcast(E2M1),
+                    lhsT_scale=wb_sc[:, a * P : (a + 1) * P],
+                    rhs=h_codes[h][:].bitcast(E5M2),
+                    rhs_scale=h_sc[h][:],
+                    start=True,
+                    stop=True,
+                )
+        for h in range(JT):
+            nc.vector.tensor_tensor(res[h][:], p_ps[h][:], looked[:, :, h * P : (h + 1) * P], ALU.mult)
+            nc.sync.dma_start(out_view[:, :, h * P : (h + 1) * P], res[h][:])

@@ -58,8 +58,8 @@ def tile_list_rows_pickgaps_grouppeaks_timeslook_kernel(
         nc.vector.memset(wb_sc[:].bitcast(I32), 0)
 
         x_view = xf.rearrange("(p i) t -> p i t", i=PACK)
-        nc.sync.dma_start(second[:], offs2)
         nc.sync.dma_start(x_rows[0][:], x_view[:, 0, :])
+        nc.sync.dma_start(second[:], offs2)
         nc.sync.dma_start(first[:], offs)
         for i in range(1, PACK):
             nc.sync.dma_start(x_rows[i][:], x_view[:, i, :])
@@ -120,8 +120,6 @@ def tile_list_rows_pickgaps_grouppeaks_timeslook_kernel(
         quantise_gaps(1)
 
         looked = keep.tile([P, NT, J], F32, name="looked")
-        for a in range(NT):
-            nc.scalar.activation(looked[:, a, :], tz_rows[a][:].indirect(third[:]), ACT.Copy)
 
         a_ps = [[psum.tile([P, HALF], F32, name="a_ps%d%d" % (h, s)) for s in range(2)] for h in range(JT)]
         peaks = [keep.tile([P, G], F32, name="peaks%d" % h) for h in range(JT)]
@@ -138,33 +136,57 @@ def tile_list_rows_pickgaps_grouppeaks_timeslook_kernel(
                     stop=True,
                 )
         GH = G // 2
-        for h in range(JT):
-            for s in range(2):
-                nc.vector.tensor_reduce(
-                    peaks[h][:, s * GH : (s + 1) * GH],
-                    a_ps[h][s][:].rearrange("p (g e) -> p g e", e=BUNDLE),
-                    AXIS.X,
-                    ALU.max,
-                )
-        for h in range(JT):
-            for pair in range(2):
-                for s in range(2):
-                    nc.vector.scalar_tensor_tensor(
-                        above[h][:, 2 * pair : 2 * pair + 2, s * 64 : (s + 1) * 64].rearrange("p i q -> p q i"),
-                        peaks[h][:, s * GH : (s + 1) * GH].unsqueeze(2).to_broadcast([P, GH, 4]),
-                        -0.5,
-                        a_ps[h][s][:].rearrange("p (q i) -> p q i", i=PACK)[:, :, 2 * pair : 2 * pair + 2],
-                        ALU.mult,
-                        ALU.add,
-                    )
-
+        QH = P // 2
         turned = [psum.tile([P, PACK, P], F32, name="turned%d" % h) for h in range(JT)]
         h_bf = [keep.tile([P, P * PACK], BF16, name="h_bf%d" % h, align_bytes=64) for h in range(JT)]
         h_codes = [keep.tile([P, P], U32, name="h_codes%d" % h, align_bytes=64) for h in range(JT)]
         h_sc = [keep.tile([P, P], U8, name="h_sc%d" % h, align_bytes=64) for h in range(JT)]
-        for h in range(JT):
-            for i in range(PACK):
-                nc.tensor.transpose(turned[h][:, i, :], above[h][:, i, :], ident[:])
+
+        def find_peaks(h, s):
+            nc.vector.tensor_reduce(
+                peaks[h][:, s * GH : (s + 1) * GH],
+                a_ps[h][s][:].rearrange("p (g e) -> p g e", e=BUNDLE),
+                AXIS.X,
+                ALU.max,
+            )
+
+        def fetch_sums(s):
+            nc.scalar.activation(
+                above[0][:, :, s * QH : (s + 1) * QH],
+                a_ps[0][s][:].rearrange("p (q i) -> p i q", i=PACK),
+                ACT.Copy,
+            )
+
+        for s in range(2):
+            find_peaks(0, s)
+        fetch_sums(0)
+        lowered = keep.tile([P, P], F32, name="lowered")
+        nc.scalar.activation(
+            lowered[:].rearrange("p (g e) -> p g e", e=2),
+            peaks[0][:].unsqueeze(2).to_broadcast([P, G, 2]),
+            ACT.Copy,
+            scale=-0.5,
+        )
+        fetch_sums(1)
+        for i in range(PACK):
+            nc.tensor.matmul(turned[0][:, i, :], lowered[:], ident[:], start=(i == 0), stop=False, is_transpose=True)
+        for i in range(PACK):
+            nc.tensor.matmul(turned[0][:, i, :], above[0][:, i, :], ident[:], start=False, stop=(i == PACK - 1), is_transpose=True)
+
+        for s in range(2):
+            find_peaks(1, s)
+        for pair in range(2):
+            for s in range(2):
+                nc.vector.scalar_tensor_tensor(
+                    above[1][:, 2 * pair : 2 * pair + 2, s * QH : (s + 1) * QH].rearrange("p i q -> p q i"),
+                    peaks[1][:, s * GH : (s + 1) * GH].unsqueeze(2).to_broadcast([P, GH, 4]),
+                    -0.5,
+                    a_ps[1][s][:].rearrange("p (q i) -> p q i", i=PACK)[:, :, 2 * pair : 2 * pair + 2],
+                    ALU.mult,
+                    ALU.add,
+                )
+        for i in range(PACK):
+            nc.tensor.transpose(turned[1][:, i, :], above[1][:, i, :], ident[:])
         for h in range(JT):
             nc.vector.scalar_tensor_tensor(
                 h_bf[h][:].rearrange("p (j i) -> p j i", i=PACK),
@@ -176,6 +198,9 @@ def tile_list_rows_pickgaps_grouppeaks_timeslook_kernel(
             )
         for h in range(JT):
             nc.vector.quantize_mx(out=h_codes[h][:].bitcast(E5M2), scales=h_sc[h][:], in_=h_bf[h][:])
+
+        for a in range(NT):
+            nc.scalar.activation(looked[:, a, :], tz_rows[a][:].indirect(third[:]), ACT.Copy)
 
         p_ps = [psum.tile([P, NT, P], F32, name="p_ps%d" % h) for h in range(JT)]
         res = [keep.tile([P, NT, P], F32, name="res%d" % h) for h in range(JT)]

@@ -8,6 +8,7 @@ P = 128
 PACK = 4
 BUNDLE = R // G
 SCALAR_SLOTS = 64
+ADDED = 2
 FLOPS = 2 * J * K * R + 2 * R * N * J
 
 F32 = mybir.dt.float32
@@ -94,13 +95,16 @@ def tile_list_rows_pickgaps_grouppeaks_timeslook_kernel(
         u_bf = [keep.tile([P, P * PACK], BF16, name="u_bf%d" % h, align_bytes=64) for h in range(JT)]
         u_codes = [keep.tile([P, P], U32, name="u_codes%d" % h, align_bytes=64) for h in range(JT)]
         u_sc = [keep.tile([P, P], U8, name="u_sc%d" % h, align_bytes=64) for h in range(JT)]
-        for i in range(PACK):
-            nc.scalar.activation(
-                u_bf[0][:].rearrange("p (j i) -> p i j", i=PACK)[:, i, 0:SCALAR_SLOTS],
-                gaps[:, i, 0:SCALAR_SLOTS],
-                ACT.Copy,
-                scale=fk_sb[:, i : i + 1],
-            )
+        for j0 in (0, J - SCALAR_SLOTS):
+            h, c0 = divmod(j0, P)
+            for i in range(PACK):
+                nc.scalar.activation(
+                    u_bf[h][:].rearrange("p (j i) -> p i j", i=PACK)[:, i, c0 : c0 + SCALAR_SLOTS],
+                    gaps[:, i, j0 : j0 + SCALAR_SLOTS],
+                    ACT.Copy,
+                    scale=fk_sb[:, i : i + 1],
+                )
+
         def weave(j0):
             h, c0 = divmod(j0, P)
             nc.vector.tensor_tensor(
@@ -116,7 +120,6 @@ def tile_list_rows_pickgaps_grouppeaks_timeslook_kernel(
         weave(64)
         weave(128)
         quantise_gaps(0)
-        weave(192)
         quantise_gaps(1)
 
         looked = keep.tile([P, NT, J], F32, name="looked")
@@ -152,8 +155,8 @@ def tile_list_rows_pickgaps_grouppeaks_timeslook_kernel(
 
         def fetch_sums(s):
             nc.scalar.activation(
-                above[0][:, :, s * QH : (s + 1) * QH],
-                a_ps[0][s][:].rearrange("p (q i) -> p i q", i=PACK),
+                above[0][:, 0:ADDED, s * QH : (s + 1) * QH],
+                a_ps[0][s][:].rearrange("p (q i) -> p i q", i=PACK)[:, 0:ADDED, :],
                 ACT.Copy,
             )
 
@@ -168,25 +171,32 @@ def tile_list_rows_pickgaps_grouppeaks_timeslook_kernel(
             scale=-0.5,
         )
         fetch_sums(1)
-        for i in range(PACK):
+        for i in range(ADDED):
             nc.tensor.matmul(turned[0][:, i, :], lowered[:], ident[:], start=(i == 0), stop=False, is_transpose=True)
-        for i in range(PACK):
-            nc.tensor.matmul(turned[0][:, i, :], above[0][:, i, :], ident[:], start=False, stop=(i == PACK - 1), is_transpose=True)
+        for i in range(ADDED):
+            nc.tensor.matmul(
+                turned[0][:, i, :], above[0][:, i, :], ident[:], start=False, stop=(i == ADDED - 1), is_transpose=True
+            )
 
-        for s in range(2):
-            find_peaks(1, s)
-        for pair in range(2):
+        def lower(h, i0, i1):
             for s in range(2):
                 nc.vector.scalar_tensor_tensor(
-                    above[1][:, 2 * pair : 2 * pair + 2, s * QH : (s + 1) * QH].rearrange("p i q -> p q i"),
-                    peaks[1][:, s * GH : (s + 1) * GH].unsqueeze(2).to_broadcast([P, GH, 4]),
+                    above[h][:, i0:i1, s * QH : (s + 1) * QH].rearrange("p i q -> p q i"),
+                    peaks[h][:, s * GH : (s + 1) * GH].unsqueeze(2).to_broadcast([P, GH, 2 * (i1 - i0)]),
                     -0.5,
-                    a_ps[1][s][:].rearrange("p (q i) -> p q i", i=PACK)[:, :, 2 * pair : 2 * pair + 2],
+                    a_ps[h][s][:].rearrange("p (q i) -> p q i", i=PACK)[:, :, i0:i1],
                     ALU.mult,
                     ALU.add,
                 )
-        for i in range(PACK):
-            nc.tensor.transpose(turned[1][:, i, :], above[1][:, i, :], ident[:])
+            for i in range(i0, i1):
+                nc.tensor.transpose(turned[h][:, i, :], above[h][:, i, :], ident[:])
+
+        for s in range(2):
+            find_peaks(1, s)
+        lower(0, ADDED, PACK)
+        lower(1, 0, 2)
+        lower(1, 2, 3)
+        lower(1, 3, 4)
         for h in range(JT):
             nc.vector.scalar_tensor_tensor(
                 h_bf[h][:].rearrange("p (j i) -> p j i", i=PACK),

from contextlib import ExitStack

import concourse.mybir as mybir
from concourse.masks import make_identity

K, T, J, R, G, N, Z = 512, 512, 256, 512, 64, 256, 512
P = 128
PACK = 4
BUNDLE = R // G
SCALAR_SLOTS = 64
ADDED = 2
FLOPS = 2 * J * K * R + 2 * R * N * J

F32 = mybir.dt.float32
BF16 = mybir.dt.bfloat16
I32 = mybir.dt.int32
U32 = mybir.dt.uint32
U16 = mybir.dt.uint16
U8 = mybir.dt.uint8
E4M3 = mybir.dt.float8_e4m3fn_x4
E5M2 = mybir.dt.float8_e5m2_x4
E2M1 = mybir.dt.float4_e2m1fn_x4
ALU = mybir.AluOpType
ACT = mybir.ActivationFunctionType
AXIS = mybir.AxisListType


def tile_list_rows_pickgaps_grouppeaks_timeslook_kernel(
    tc, xf, fk, w_words, w_scales, us, wb_words, wb_scales, tz, offs, offs2, offs3, out
):
    nc = tc.nc
    JT = J // P
    NT = N // P
    HALF = R // 2

    with ExitStack() as ctx:
        keep = ctx.enter_context(tc.tile_pool(name="keep", bufs=1))
        psum = ctx.enter_context(tc.psum_pool(name="psum", bufs=1))

        first = keep.tile([P, J // 16], U16, name="first")
        second = keep.tile([P, J // 16], U16, name="second")
        third = keep.tile([P, J // 16], U16, name="third")
        x_rows = [keep.tile([P, T], F32, name="x_rows%d" % i) for i in range(PACK)]
        fk_sb = keep.tile([P, PACK], F32, name="fk_sb")
        us_sb = keep.tile([P, PACK], F32, name="us_sb")
        w_sb = keep.tile([P, 2 * R], U8, name="w_sb", align_bytes=64)
        wb_sb = keep.tile([P, 2 * N], U8, name="wb_sb", align_bytes=64)
        w_sc = keep.tile([P, R], U8, name="w_sc", align_bytes=64)
        wb_sc = keep.tile([P, N], U8, name="wb_sc", align_bytes=64)
        tz_rows = [keep.tile([P, Z], F32, name="tz_rows%d" % a) for a in range(NT)]
        ident = keep.tile([P, P], F32, name="ident")

        warm = keep.tile([P, 1], F32, name="warm")
        warmed = keep.tile([P, 1], F32, name="warmed")
        nc.vector.memset(warm[:], 0.0)
        nc.scalar.activation(warmed[:], warm[:], ACT.Copy)
        make_identity(nc, ident[:])
        nc.vector.memset(w_sc[:].bitcast(I32), 0)
        nc.vector.memset(wb_sc[:].bitcast(I32), 0)

        x_view = xf.rearrange("(p i) t -> p i t", i=PACK)
        nc.sync.dma_start(x_rows[0][:], x_view[:, 0, :])
        nc.sync.dma_start(second[:], offs2)
        nc.sync.dma_start(first[:], offs)
        for i in range(1, PACK):
            nc.sync.dma_start(x_rows[i][:], x_view[:, i, :])
        nc.sync.dma_start(fk_sb[:], fk.rearrange("(p i) o -> p (i o)", i=PACK))
        nc.sync.dma_start(w_sb[:].bitcast(I32), w_words[0].bitcast(I32))
        for q in range(4):
            nc.sync.dma_start(
                w_sc[32 * q : 32 * q + 4, :].bitcast(I32), w_scales[0, 4 * q : 4 * q + 4, :].bitcast(I32)
            )
        nc.sync.dma_start(us_sb[:], us.rearrange("o (p i) -> p (o i)", i=PACK))
        nc.sync.dma_start(third[:], offs3)
        for a in range(NT):
            nc.sync.dma_start(tz_rows[a][:], tz[a * P : (a + 1) * P, :])
        nc.sync.dma_start(wb_sb[:].bitcast(I32), wb_words[0].bitcast(I32))
        for q in range(4):
            nc.sync.dma_start(
                wb_sc[32 * q : 32 * q + 4, :].bitcast(I32), wb_scales[0, 4 * q : 4 * q + 4, :].bitcast(I32)
            )

        taken = keep.tile([P, PACK, J], F32, name="taken")
        gaps = keep.tile([P, PACK, J], F32, name="gaps")
        for i in range(PACK):
            width = P if i in (0, PACK - 1) else J
            for j0 in range(0, J, width):
                slots = slice(j0, j0 + width)
                cols = slice(j0 // 16, (j0 + width) // 16)
                nc.scalar.activation(taken[:, i, slots], x_rows[i][:].indirect(second[:, cols]), ACT.Copy)
                nc.vector.tensor_tensor(
                    gaps[:, i, slots], x_rows[i][:].indirect(first[:, cols]), taken[:, i, slots], ALU.subtract
                )

        u_bf = [keep.tile([P, P * PACK], BF16, name="u_bf%d" % h, align_bytes=64) for h in range(JT)]
        u_codes = [keep.tile([P, P], U32, name="u_codes%d" % h, align_bytes=64) for h in range(JT)]
        u_sc = [keep.tile([P, P], U8, name="u_sc%d" % h, align_bytes=64) for h in range(JT)]
        for j0 in (0, J - SCALAR_SLOTS):
            h, c0 = divmod(j0, P)
            for i in range(PACK):
                nc.scalar.activation(
                    u_bf[h][:].rearrange("p (j i) -> p i j", i=PACK)[:, i, c0 : c0 + SCALAR_SLOTS],
                    gaps[:, i, j0 : j0 + SCALAR_SLOTS],
                    ACT.Copy,
                    scale=fk_sb[:, i : i + 1],
                )

        def weave(j0):
            h, c0 = divmod(j0, P)
            nc.vector.tensor_tensor(
                u_bf[h][:, PACK * c0 : PACK * (c0 + 64)].rearrange("p (c s i) -> p c i s", s=4, i=PACK),
                gaps[:, :, j0 : j0 + 64].rearrange("p i (c s) -> p c i s", s=4),
                fk_sb[:].unsqueeze(1).unsqueeze(3).to_broadcast([P, 16, PACK, 4]),
                ALU.mult,
            )

        def quantise_gaps(h):
            nc.vector.quantize_mx(out=u_codes[h][:].bitcast(E4M3), scales=u_sc[h][:], in_=u_bf[h][:])

        weave(64)
        weave(128)
        quantise_gaps(0)
        quantise_gaps(1)

        looked = keep.tile([P, NT, J], F32, name="looked")

        a_ps = [[psum.tile([P, HALF], F32, name="a_ps%d%d" % (h, s)) for s in range(2)] for h in range(JT)]
        peaks = [keep.tile([P, G], F32, name="peaks%d" % h) for h in range(JT)]
        above = [keep.tile([P, PACK, P], F32, name="above%d" % h) for h in range(JT)]
        for h in range(JT):
            for s in range(2):
                nc.tensor.matmul_mx(
                    out=a_ps[h][s][:],
                    lhsT=u_codes[h][:].bitcast(E4M3),
                    lhsT_scale=u_sc[h][:],
                    rhs=w_sb[:, 2 * s * HALF : 2 * (s + 1) * HALF].bitcast(E2M1),
                    rhs_scale=w_sc[:, s * HALF : (s + 1) * HALF],
                    start=True,
                    stop=True,
                )
        GH = G // 2
        QH = P // 2
        turned = [psum.tile([P, PACK, P], F32, name="turned%d" % h) for h in range(JT)]
        h_bf = [keep.tile([P, P * PACK], BF16, name="h_bf%d" % h, align_bytes=64) for h in range(JT)]
        h_codes = [keep.tile([P, P], U32, name="h_codes%d" % h, align_bytes=64) for h in range(JT)]
        h_sc = [keep.tile([P, P], U8, name="h_sc%d" % h, align_bytes=64) for h in range(JT)]

        def find_peaks(h, s):
            nc.vector.tensor_reduce(
                peaks[h][:, s * GH : (s + 1) * GH],
                a_ps[h][s][:].rearrange("p (g e) -> p g e", e=BUNDLE),
                AXIS.X,
                ALU.max,
            )

        def fetch_sums(s):
            nc.scalar.activation(
                above[0][:, 0:ADDED, s * QH : (s + 1) * QH],
                a_ps[0][s][:].rearrange("p (q i) -> p i q", i=PACK)[:, 0:ADDED, :],
                ACT.Copy,
            )

        for s in range(2):
            find_peaks(0, s)
        fetch_sums(0)
        lowered = keep.tile([P, P], F32, name="lowered")
        nc.scalar.activation(
            lowered[:].rearrange("p (g e) -> p g e", e=2),
            peaks[0][:].unsqueeze(2).to_broadcast([P, G, 2]),
            ACT.Copy,
            scale=-0.5,
        )
        fetch_sums(1)
        for i in range(ADDED):
            nc.tensor.matmul(turned[0][:, i, :], lowered[:], ident[:], start=(i == 0), stop=False, is_transpose=True)
        for i in range(ADDED):
            nc.tensor.matmul(
                turned[0][:, i, :], above[0][:, i, :], ident[:], start=False, stop=(i == ADDED - 1), is_transpose=True
            )

        def lower(h, i0, i1):
            for s in range(2):
                nc.vector.scalar_tensor_tensor(
                    above[h][:, i0:i1, s * QH : (s + 1) * QH].rearrange("p i q -> p q i"),
                    peaks[h][:, s * GH : (s + 1) * GH].unsqueeze(2).to_broadcast([P, GH, 2 * (i1 - i0)]),
                    -0.5,
                    a_ps[h][s][:].rearrange("p (q i) -> p q i", i=PACK)[:, :, i0:i1],
                    ALU.mult,
                    ALU.add,
                )
            for i in range(i0, i1):
                nc.tensor.transpose(turned[h][:, i, :], above[h][:, i, :], ident[:])

        for s in range(2):
            find_peaks(1, s)
        lower(0, ADDED, PACK)
        lower(1, 0, 2)
        lower(1, 2, 3)
        lower(1, 3, 4)
        for h in range(JT):
            nc.vector.scalar_tensor_tensor(
                h_bf[h][:].rearrange("p (j i) -> p j i", i=PACK),
                turned[h][:].rearrange("p i j -> p j i"),
                0.0,
                us_sb[:].unsqueeze(1).to_broadcast([P, P, PACK]),
                ALU.max,
                ALU.mult,
            )
        for h in range(JT):
            nc.vector.quantize_mx(out=h_codes[h][:].bitcast(E5M2), scales=h_sc[h][:], in_=h_bf[h][:])

        for a in range(NT):
            nc.scalar.activation(looked[:, a, :], tz_rows[a][:].indirect(third[:]), ACT.Copy)

        p_ps = [psum.tile([P, NT, P], F32, name="p_ps%d" % h) for h in range(JT)]
        res = [keep.tile([P, NT, P], F32, name="res%d" % h) for h in range(JT)]
        out_view = out.rearrange("(a p) j -> p a j", p=P)
        for h in range(JT):
            for a in range(NT):
                nc.tensor.matmul_mx(
                    out=p_ps[h][:, a, :],
                    lhsT=wb_sb[:, 2 * a * P : 2 * (a + 1) * P].bitcast(E2M1),
                    lhsT_scale=wb_sc[:, a * P : (a + 1) * P],
                    rhs=h_codes[h][:].bitcast(E5M2),
                    rhs_scale=h_sc[h][:],
                    start=True,
                    stop=True,
                )
        for h in range(JT):
            nc.vector.tensor_tensor(res[h][:], p_ps[h][:], looked[:, :, h * P : (h + 1) * P], ALU.mult)
            nc.sync.dma_start(out_view[:, :, h * P : (h + 1) * P], res[h][:])
